import numpy as np
import ml_dtypes


def mxq(x, axis, fmt="e4m3"):
    dtype, down = {"e4m3": (ml_dtypes.float8_e4m3fn, 7), "e5m2": (ml_dtypes.float8_e5m2, 14)}[fmt]
    v = np.moveaxis(np.asarray(x, np.float32).astype(ml_dtypes.bfloat16).astype(np.float64), axis, -1)
    blocks = v.reshape(v.shape[:-1] + (-1, 32))
    amax = np.abs(blocks).max(-1, keepdims=True)
    byte = np.maximum(np.where(amax > 0, np.frexp(amax)[1] - 1 + 127, 0) - down, 1)
    scale = np.exp2(byte - 127.0)
    codes = (blocks / scale).astype(np.float32).astype(dtype).astype(np.float64)
    return np.moveaxis((codes * scale).reshape(v.shape), -1, axis)


WIDE = False


def mx_kscale(k):
    if not WIDE:
        return np.ones(k)
    levels = np.array([10, -10, 5, -5, 0])
    if k % 512:
        return np.exp2(np.random.permutation(np.resize(levels, k // 32))).repeat(32)
    a = np.empty((k // 512, 16))
    for p in range(k // 512):
        a[p, :8] = np.random.permutation(np.resize(levels, 8))
        for g in range(8):
            far = levels[np.abs(levels - a[p, g]) >= 10]
            a[p, g + 8] = far[np.random.randint(len(far))]
    return np.exp2(a.ravel()).repeat(32)


def f64(x):
    return np.asarray(x).astype(np.float64)


def striped(idx):
    return np.tile(np.asarray(idx).reshape(-1, 16).T, (8, 1)).astype(np.uint16)


def unstriped(offs):
    return offs[:16].T.reshape(-1).astype(np.int64)


E2M1 = np.array([0.0, 0.5, 1.0, 1.5, 2.0, 3.0, 4.0, 6.0, -0.0, -0.5, -1.0, -1.5, -2.0, -3.0, -4.0, -6.0])


def pack_weight(w, fmt):
    k, n = w.shape
    w = f64(np.asarray(w, np.float32).astype(ml_dtypes.bfloat16)).reshape(k // 32, 32, n)
    amax = np.abs(w).max(1)
    if fmt == "e4m3":
        byte = np.frexp(amax)[1] - 1 + 127 - 7
    else:
        mant, ex = np.frexp(amax / 6.0)
        byte = np.where(mant > 0.5, ex, ex - 1) + 127
    byte = np.clip(np.where(amax > 0, byte, 1), 1, 254)
    scaled = (w * np.exp2(127.0 - byte)[:, None, :]).reshape(k, n).astype(np.float32)
    by_word = np.ascontiguousarray(scaled.reshape(k // 512, 128, 4, n).transpose(0, 1, 3, 2))
    if fmt == "e4m3":
        words = by_word.astype(ml_dtypes.float8_e4m3fn).view(np.uint8)
    else:
        c = by_word.astype(ml_dtypes.float4_e2m1fn).view(np.uint8) & 0xF
        words = (c[..., 0::2] | (c[..., 1::2] << 4)).reshape(k // 512, 128, 2 * n)
    return np.ascontiguousarray(words), np.ascontiguousarray(byte.astype(np.uint8).reshape(k // 512, 16, n))


def unpack_weight(words, scales, fmt):
    g, _, n = scales.shape
    words = np.ascontiguousarray(words).reshape(g, 128, n, -1)
    if fmt == "e4m3":
        vals = words.view(ml_dtypes.float8_e4m3fn).astype(np.float64)
    else:
        nib = np.empty((g, 128, n, 4), np.uint8)
        nib[..., 0::2] = words & 0xF
        nib[..., 1::2] = words >> 4
        vals = E2M1[nib]
    vals = vals * np.repeat(np.exp2(scales.astype(np.float64) - 127.0), 8, axis=1)[..., None]
    return vals.transpose(0, 1, 3, 2).reshape(g * 512, n)


def bf(x):
    return np.asarray(x, np.float32).astype(ml_dtypes.bfloat16)


def planes(Y):
    r, m = Y.shape
    b = f64(bf(Y)).reshape(r // 32, 32, m)
    amax = np.abs(b).max(1)
    byte = np.clip(np.where(amax > 0, np.frexp(amax)[1] - 1 + 127 - 7, 1), 1, 254)
    codes = (b * np.exp2(127.0 - byte)[:, None, :]).reshape(r, m).astype(np.float32).astype(ml_dtypes.float8_e4m3fn).view(np.uint8)
    words = codes.reshape(r // 512, 128, 4, m).transpose(0, 1, 3, 2)
    return np.ascontiguousarray(words), np.ascontiguousarray(byte.astype(np.uint8).reshape(r // 512, 16, m))


D, T, I, Q, E, U = 512, 2048, 512, 256, 512, 512


def setup_inputs():
    n = np.random.standard_normal
    idx = np.random.permutation(T)[:I]
    idx2 = np.random.randint(0, U, I)
    fd = mx_kscale(D)
    fi = mx_kscale(I)
    ti = np.ones(T)
    ti[idx] = fi
    keysp = pack_weight(n((D, T)) / fd[:, None], "e2m1")
    return {
        "query": (n((D, Q)) * 0.25 / np.sqrt(D) * fd[:, None]).astype(np.float32),
        "keys_words": keysp[0],
        "keys_scales": keysp[1],
        "pquery": (n((D, Q)) * 0.5 / np.sqrt(D) * fd[:, None]).astype(np.float32),
        "place": (n((D, U)) / fd[:, None]).astype(np.float32),
        "size": (np.random.uniform(0.5, 2.0, (1, I)) * fi).astype(np.float32),
        "vals": (n((E, T)) / ti).astype(np.float32),
        "offs": striped(idx),
        "offs2": striped(idx2),
    }


def reference(query, keys_words, keys_scales, pquery, place, size, vals, offs, offs2):
    idx = unstriped(offs)
    idx2 = unstriped(offs2)
    keysu = unpack_weight(keys_words, keys_scales, "e2m1")
    queryq = mxq(f64(query), 0, "e4m3")
    keysidxg = keysu[:, idx]
    a = queryq.T @ keysidxg
    pqueryq = mxq(f64(pquery), 0, "e4m3")
    placeq = mxq(f64(place), 0, "e4m3")
    b = pqueryq.T @ placeq
    s = a * (b[:, idx2] + 1.0)
    p = np.exp(s - np.max(s, axis=1, keepdims=True))
    w = p * f64(size) / np.sum(p, axis=1, keepdims=True)
    wt = w.T
    vt = f64(vals)[:, idx].T
    vtq = mxq(vt, 0, "e4m3")
    wtq = mxq(wt, 0, "e4m3")
    o = vtq.T @ wtq
    words, scales = planes(o)
    return o, words, scales

@@ -1,0 +1,199 @@
+from contextlib import ExitStack
+
+import concourse.mybir as mybir
+from concourse.masks import make_identity
+
+D, T, I, Q, E, U = 512, 2048, 512, 256, 512, 512
+FLOPS = 2 * D * Q * I + 2 * D * Q * U + 2 * I * E * Q
+
+F32 = mybir.dt.float32
+BF16 = mybir.dt.bfloat16
+I32 = mybir.dt.int32
+U32 = mybir.dt.uint32
+U16 = mybir.dt.uint16
+U8 = mybir.dt.uint8
+FP8X4 = mybir.dt.float8_e4m3fn_x4
+FP4X4 = mybir.dt.float4_e2m1fn_x4
+ALU = mybir.AluOpType
+ACT = mybir.ActivationFunctionType
+
+P = 128
+PACK = 4
+HALVES = Q // P
+B_WINDOW = 704
+
+
+def tile_attend_productscores_pl_kernel(tc, query, keys_words, keys_scales, pquery, place, size, vals, offs, offs2,
+                                         out_0, out_1, out_2):
+    nc = tc.nc
+    with ExitStack() as ctx:
+        sb = ctx.enter_context(tc.tile_pool(name="sb", bufs=1))
+        ps = ctx.enter_context(tc.psum_pool(name="ps", bufs=1))
+
+        def interleave(engine_copy, dst, src):
+            engine_copy(out=dst.rearrange("p (c i) t -> p c t i", i=4), in_=src.rearrange("p t (c i) -> p c t i", i=4))
+
+        def quantize(name, grouped, width):
+            codes = sb.tile([P, width], U32, name=name + "_codes", align_bytes=64)
+            scales = sb.tile([P, width], U8, name=name + "_scales", align_bytes=64)
+            nc.vector.quantize_mx(out=codes[:].bitcast(FP8X4), scales=scales[:], in_=grouped.rearrange("p c t -> p (c t)"))
+            return codes, scales
+
+        slots = sb.tile([P, I // 16], U16, name="slots")
+        places = sb.tile([P, I // 16], U16, name="places")
+        key_scales = sb.tile([P, T], U8, name="key_scales", align_bytes=64)
+        key_words = sb.tile([P, T], U16, name="key_words", align_bytes=64)
+        pq_raw = sb.tile([P, PACK, Q], F32, name="pq_raw")
+        q_raw = sb.tile([P, PACK, Q], F32, name="q_raw")
+        place_raw = [sb.tile([P, PACK, U // 2], F32, name="place_raw%d" % g) for g in range(2)]
+        size_raw = sb.tile([P, PACK], F32, name="size_raw")
+        val_planes = [sb.tile([P, T], F32, name="val_plane%d" % j) for j in range(PACK)]
+
+        nc.vector.memset(key_scales[:].bitcast(I32), 0)
+        nc.sync.dma_start(slots[:], offs)
+        nc.sync.dma_start(out=pq_raw[:], in_=pquery.rearrange("(p t) q -> p t q", t=PACK))
+        for quad in range(4):
+            nc.scalar.dma_start(out=key_scales[32 * quad:32 * quad + 4, :].bitcast(I32),
+                                in_=keys_scales[0, 4 * quad:4 * quad + 4, :].bitcast(I32))
+        place_rows = place.rearrange("(p t) u -> p t u", t=PACK)
+        for g in range(2):
+            nc.sync.dma_start(out=place_raw[g][:], in_=place_rows[:, :, g * (U // 2):(g + 1) * (U // 2)])
+        nc.sync.dma_start(out=key_words[:].bitcast(I32), in_=keys_words[0].bitcast(I32))
+        nc.sync.dma_start(places[:], offs2)
+        nc.sync.dma_start(out=q_raw[:], in_=query.rearrange("(p t) q -> p t q", t=PACK))
+        nc.sync.dma_start(out=size_raw[:], in_=size[0].rearrange("(p t) -> p t", t=PACK))
+        val_rows = vals.rearrange("(m j) t -> m j t", j=PACK)
+        for j in range(PACK):
+            nc.sync.dma_start(out=val_planes[j][:], in_=val_rows[:, j, :])
+
+        warm = sb.tile([P, 8], F32, name="warm")
+        warm_out = sb.tile([P, 8], F32, name="warm_out")
+        nc.gpsimd.memset(warm[:], 0.0)
+        nc.scalar.activation(out=warm_out[:], in_=warm[:], func=ACT.Exp)
+        ident = sb.tile([P, P], F32, name="ident")
+        make_identity(nc, ident[:])
+        b_sb = [sb.tile([P, B_WINDOW], F32, name="b_sb%d" % h) for h in range(HALVES)]
+        for h in range(HALVES):
+            nc.gpsimd.memset(b_sb[h][:, U:], 0.0)
+
+        ks_g = sb.tile([P, I], U8, name="ks_g", align_bytes=64)
+        nc.vector.tensor_copy(ks_g[:], key_scales[:].indirect(slots[:]))
+
+        pq_grp = sb.tile([P, Q, PACK], BF16, name="pq_grp", align_bytes=64)
+        interleave(nc.scalar.copy, pq_grp[:], pq_raw[:])
+        place_mx = []
+        for g in range(2):
+            grp = sb.tile([P, U // 2, PACK], BF16, name="place_grp%d" % g, align_bytes=64)
+            interleave(nc.vector.tensor_copy, grp[:], place_raw[g][:])
+            if g == 0:
+                pq_codes, pq_scales = quantize("pq", pq_grp[:], Q)
+            place_mx.append(quantize("place%d" % g, grp[:], U // 2))
+
+        kw_g = sb.tile([P, I], U16, name="kw_g", align_bytes=64)
+        nc.vector.tensor_copy(kw_g[:], key_words[:].indirect(slots[:]))
+
+        for h in range(HALVES):
+            cols = slice(h * P, (h + 1) * P)
+            b_ps = ps.tile([P, U], F32, name="b_ps%d" % h, tag="b_or_out", bufs=2)
+            for g in range(2):
+                nc.tensor.matmul_mx(out=b_ps[:, g * (U // 2):(g + 1) * (U // 2)],
+                                    lhsT=pq_codes[:, cols].bitcast(FP8X4), lhsT_scale=pq_scales[:, cols],
+                                    rhs=place_mx[g][0][:].bitcast(FP8X4), rhs_scale=place_mx[g][1][:],
+                                    start=True, stop=True)
+            nc.scalar.copy(out=b_sb[h][:, :U], in_=b_ps[:])
+
+        size_ps = ps.tile([P, PACK, P], F32, name="size_ps")
+        for t in range(PACK):
+            nc.tensor.transpose(size_ps[:, t, :], size_raw[:, t:t + 1].to_broadcast([P, P]), ident[:])
+
+        a_ps, b_g = [], []
+        for h in range(HALVES):
+            gathered = sb.tile([P, I], F32, name="b_g%d" % h)
+            nc.vector.tensor_copy(gathered[:], b_sb[h][:].indirect(places[:]))
+            b_g.append(gathered)
+            grp = sb.tile([P, P, PACK], BF16, name="q_grp%d" % h, align_bytes=64)
+            interleave(nc.scalar.copy, grp[:], q_raw[:, :, h * P:(h + 1) * P])
+            codes, scales = quantize("q%d" % h, grp[:], P)
+            bank = ps.tile([P, I], F32, name="a_ps%d" % h, tag="a_or_wt", bufs=2)
+            nc.tensor.matmul_mx(out=bank[:], lhsT=codes[:].bitcast(FP8X4), lhsT_scale=scales[:],
+                                rhs=kw_g[:].bitcast(FP4X4), rhs_scale=ks_g[:], start=True, stop=True)
+            a_ps.append(bank)
+
+        probs, sums = [], []
+        for h in range(HALVES):
+            s = sb.tile([P, I], F32, name="s%d" % h)
+            nc.vector.scalar_tensor_tensor(out=s[:], in0=b_g[h][:], scalar=1.0, in1=a_ps[h][:], op0=ALU.add, op1=ALU.mult)
+            neg_max = sb.tile([P, 1], F32, name="neg_max%d" % h)
+            nc.vector.tensor_reduce(out=neg_max[:], in_=s[:], axis=mybir.AxisListType.X, op=ALU.max, negate=True)
+            p = sb.tile([P, I], F32, name="p%d" % h)
+            total = sb.tile([P, 1], F32, name="total%d" % h)
+            nc.scalar.activation(out=p[:], in_=s[:], func=ACT.Exp, bias=neg_max[:], accum_out=total[:])
+            probs.append(p)
+            sums.append(total)
+
+        def turn(name, rows_bf16, tag, bufs):
+            words = rows_bf16[:].bitcast(F32)
+            bank = ps.tile([P, 2, P], F32, name=name + "_ps", tag=tag, bufs=bufs)
+            for u in range(2):
+                nc.tensor.transpose(bank[:, u, :], words[:, u::2], ident[:])
+            grp = sb.tile([P, P, PACK], BF16, name=name + "_grp", align_bytes=64)
+            nc.scalar.copy(out=grp[:].rearrange("p c t -> p (c t)").bitcast(F32).rearrange("p (c u) -> p c u", u=2),
+                           in_=bank[:].rearrange("p u c -> p c u"))
+            return grp
+
+        def gather_values(j):
+            v_g = sb.tile([P, I], BF16, name="v_g%d" % j, align_bytes=64)
+            nc.vector.tensor_copy(v_g[:], val_planes[j][:].indirect(slots[:]))
+            return turn("vt%d" % j, v_g, "vt", 3)
+
+        def weights(h):
+            inv = sb.tile([P, 1], F32, name="inv%d" % h)
+            nc.vector.reciprocal(out=inv[:], in_=sums[h][:])
+            w = sb.tile([P, I], BF16, name="w%d" % h, align_bytes=64)
+            nc.vector.scalar_tensor_tensor(out=w[:].rearrange("q (s t) -> q s t", t=PACK),
+                                           in0=probs[h][:].rearrange("q (s t) -> q s t", t=PACK), scalar=inv[:],
+                                           in1=size_ps[:].rearrange("q t s -> q s t"), op0=ALU.mult, op1=ALU.mult)
+            return turn("wt%d" % h, w, "a_or_wt", 2)
+
+        wt_grp0 = weights(0)
+        vt_grp0 = gather_values(0)
+        wt_grp1 = weights(1)
+        vt_grp1 = gather_values(1)
+        wt_mx = [quantize("wt0", wt_grp0[:], P)]
+        vt_mx = [quantize("vt0", vt_grp0[:], P)]
+        wt_mx.append(quantize("wt1", wt_grp1[:], P))
+        vt_grp2 = gather_values(2)
+        vt_mx.append(quantize("vt1", vt_grp1[:], P))
+        vt_grp3 = gather_values(3)
+        vt_mx.append(quantize("vt2", vt_grp2[:], P))
+        vt_mx.append(quantize("vt3", vt_grp3[:], P))
+
+        o_ps = [ps.tile([P, PACK, P], F32, name="o_ps%d" % h, tag="b_or_out", bufs=2) for h in range(HALVES)]
+        o_sb = sb.tile([P, PACK, Q], F32, name="o_sb")
+        out_rows = out_0.rearrange("(m j) q -> m j q", j=PACK)
+
+        def product(j):
+            for h in range(HALVES):
+                nc.tensor.matmul_mx(out=o_ps[h][:, j, :], lhsT=vt_mx[j][0][:].bitcast(FP8X4), lhsT_scale=vt_mx[j][1][:],
+                                    rhs=wt_mx[h][0][:].bitcast(FP8X4), rhs_scale=wt_mx[h][1][:], start=True, stop=True)
+
+        last = PACK - 1
+        for j in range(last):
+            product(j)
+        for h in range(HALVES):
+            nc.scalar.copy(out=o_sb[:, :last, h * P:(h + 1) * P], in_=o_ps[h][:, :last, :])
+        nc.sync.dma_start(out=out_rows[:, :last, :], in_=o_sb[:, :last, :])
+        product(last)
+
+        o_grp = sb.tile([P, Q, PACK], BF16, name="o_grp", align_bytes=64)
+        nc.vector.tensor_copy(out=o_grp[:, :P, :], in_=o_ps[0][:].rearrange("m j q -> m q j"))
+        nc.scalar.copy(out=o_grp[:, P:, :], in_=o_ps[1][:].rearrange("m j q -> m q j"))
+        for h in (1, 0):
+            nc.scalar.copy(out=o_sb[:, last, h * P:(h + 1) * P], in_=o_ps[h][:, last, :])
+        o_codes, o_scales = quantize("o", o_grp[:], Q)
+        nc.sync.dma_start(out=out_rows[:, last, :], in_=o_sb[:, last, :])
+        nc.sync.dma_start(out=out_1[0].rearrange("l c r -> l (c r)").bitcast(I32), in_=o_codes[:].bitcast(I32))
+        for quad in range(4):
+            queue = nc.scalar if quad % 2 else nc.sync
+            queue.dma_start(out=out_2[0, 4 * quad:4 * quad + 4, :].bitcast(I32),
+                            in_=o_scales[32 * quad:32 * quad + 4, :].bitcast(I32))

@@ -33,8 +33,8 @@ def tile_attend_productscores_pl_kernel(tc, query, keys_words, keys_scales, pque
         def interleave(engine_copy, dst, src):
             engine_copy(out=dst.rearrange("p (c i) t -> p c t i", i=4), in_=src.rearrange("p t (c i) -> p c t i", i=4))
 
-        def quantize(name, grouped, width):
-            codes = sb.tile([P, width], U32, name=name + "_codes", align_bytes=64)
+        def quantize(name, grouped, width, after=None):
+            codes = sb.tile([P, width], U32, name=name + "_codes", align_bytes=64, tag=after or name + "_codes")
             scales = sb.tile([P, width], U8, name=name + "_scales", align_bytes=64)
             nc.vector.quantize_mx(out=codes[:].bitcast(FP8X4), scales=scales[:], in_=grouped.rearrange("p c t -> p (c t)"))
             return codes, scales
@@ -47,10 +47,16 @@ def tile_attend_productscores_pl_kernel(tc, query, keys_words, keys_scales, pque
         q_raw = sb.tile([P, PACK, Q], F32, name="q_raw")
         place_raw = [sb.tile([P, PACK, U // 2], F32, name="place_raw%d" % g) for g in range(2)]
         size_raw = sb.tile([P, PACK], F32, name="size_raw")
-        val_planes = [sb.tile([P, T], F32, name="val_plane%d" % j) for j in range(PACK)]
+        val_planes = [sb.tile([P, T], F32, name="val_plane%d" % j, tag="plane%d" % j, align_bytes=64) for j in range(PACK)]
 
-        nc.vector.memset(key_scales[:].bitcast(I32), 0)
+        warm = sb.tile([P, 8], F32, name="warm")
+        warm_out = sb.tile([P, 8], F32, name="warm_out")
+        nc.gpsimd.memset(warm[:], 0.0)
+        nc.scalar.activation(out=warm_out[:], in_=warm[:], func=ACT.Exp)
+        nc.gpsimd.memset(key_scales[:].bitcast(I32), 0)
         nc.sync.dma_start(slots[:], offs)
+        nc.sync.dma_start(places[:], offs2)
+        nc.sync.dma_start(out=size_raw[:], in_=size[0].rearrange("(p t) -> p t", t=PACK))
         nc.sync.dma_start(out=pq_raw[:], in_=pquery.rearrange("(p t) q -> p t q", t=PACK))
         for quad in range(4):
             nc.scalar.dma_start(out=key_scales[32 * quad:32 * quad + 4, :].bitcast(I32),
@@ -59,55 +65,44 @@ def tile_attend_productscores_pl_kernel(tc, query, keys_words, keys_scales, pque
         for g in range(2):
             nc.sync.dma_start(out=place_raw[g][:], in_=place_rows[:, :, g * (U // 2):(g + 1) * (U // 2)])
         nc.sync.dma_start(out=key_words[:].bitcast(I32), in_=keys_words[0].bitcast(I32))
-        nc.sync.dma_start(places[:], offs2)
         nc.sync.dma_start(out=q_raw[:], in_=query.rearrange("(p t) q -> p t q", t=PACK))
-        nc.sync.dma_start(out=size_raw[:], in_=size[0].rearrange("(p t) -> p t", t=PACK))
         val_rows = vals.rearrange("(m j) t -> m j t", j=PACK)
         for j in range(PACK):
             nc.sync.dma_start(out=val_planes[j][:], in_=val_rows[:, j, :])
 
-        warm = sb.tile([P, 8], F32, name="warm")
-        warm_out = sb.tile([P, 8], F32, name="warm_out")
-        nc.gpsimd.memset(warm[:], 0.0)
-        nc.scalar.activation(out=warm_out[:], in_=warm[:], func=ACT.Exp)
         ident = sb.tile([P, P], F32, name="ident")
         make_identity(nc, ident[:])
         b_sb = [sb.tile([P, B_WINDOW], F32, name="b_sb%d" % h) for h in range(HALVES)]
         for h in range(HALVES):
             nc.gpsimd.memset(b_sb[h][:, U:], 0.0)
 
+        pq_grp = sb.tile([P, Q, PACK], BF16, name="pq_grp", align_bytes=64)
+        interleave(nc.vector.tensor_copy, pq_grp[:], pq_raw[:])
+        pq_codes, pq_scales = quantize("pq", pq_grp[:], Q)
         ks_g = sb.tile([P, I], U8, name="ks_g", align_bytes=64)
         nc.vector.tensor_copy(ks_g[:], key_scales[:].indirect(slots[:]))
-
-        pq_grp = sb.tile([P, Q, PACK], BF16, name="pq_grp", align_bytes=64)
-        interleave(nc.scalar.copy, pq_grp[:], pq_raw[:])
-        place_mx = []
-        for g in range(2):
-            grp = sb.tile([P, U // 2, PACK], BF16, name="place_grp%d" % g, align_bytes=64)
-            interleave(nc.vector.tensor_copy, grp[:], place_raw[g][:])
-            if g == 0:
-                pq_codes, pq_scales = quantize("pq", pq_grp[:], Q)
-            place_mx.append(quantize("place%d" % g, grp[:], U // 2))
+        place_grp = [sb.tile([P, U // 2, PACK], BF16, name="place_grp%d" % g, align_bytes=64) for g in range(2)]
+        interleave(nc.scalar.copy, place_grp[0][:], place_raw[0][:])
+        interleave(nc.vector.tensor_copy, place_grp[1][:], place_raw[1][:])
+        place_mx = [quantize("place%d" % g, place_grp[g][:], U // 2) for g in range(2)]
 
         kw_g = sb.tile([P, I], U16, name="kw_g", align_bytes=64)
         nc.vector.tensor_copy(kw_g[:], key_words[:].indirect(slots[:]))
 
+        b_ps = []
         for h in range(HALVES):
             cols = slice(h * P, (h + 1) * P)
-            b_ps = ps.tile([P, U], F32, name="b_ps%d" % h, tag="b_or_out", bufs=2)
+            bank = ps.tile([P, U], F32, name="b_ps%d" % h, tag="b_or_out", bufs=2)
             for g in range(2):
-                nc.tensor.matmul_mx(out=b_ps[:, g * (U // 2):(g + 1) * (U // 2)],
+                nc.tensor.matmul_mx(out=bank[:, g * (U // 2):(g + 1) * (U // 2)],
                                     lhsT=pq_codes[:, cols].bitcast(FP8X4), lhsT_scale=pq_scales[:, cols],
                                     rhs=place_mx[g][0][:].bitcast(FP8X4), rhs_scale=place_mx[g][1][:],
                                     start=True, stop=True)
-            nc.scalar.copy(out=b_sb[h][:, :U], in_=b_ps[:])
-
-        size_ps = ps.tile([P, PACK, P], F32, name="size_ps")
-        for t in range(PACK):
-            nc.tensor.transpose(size_ps[:, t, :], size_raw[:, t:t + 1].to_broadcast([P, P]), ident[:])
+            b_ps.append(bank)
 
         a_ps, b_g = [], []
         for h in range(HALVES):
+            nc.scalar.copy(out=b_sb[h][:, :U], in_=b_ps[h][:])
             gathered = sb.tile([P, I], F32, name="b_g%d" % h)
             nc.vector.tensor_copy(gathered[:], b_sb[h][:].indirect(places[:]))
             b_g.append(gathered)
@@ -119,79 +114,88 @@ def tile_attend_productscores_pl_kernel(tc, query, keys_words, keys_scales, pque
                                 rhs=kw_g[:].bitcast(FP4X4), rhs_scale=ks_g[:], start=True, stop=True)
             a_ps.append(bank)
 
-        probs, sums = [], []
-        for h in range(HALVES):
-            s = sb.tile([P, I], F32, name="s%d" % h)
-            nc.vector.scalar_tensor_tensor(out=s[:], in0=b_g[h][:], scalar=1.0, in1=a_ps[h][:], op0=ALU.add, op1=ALU.mult)
-            neg_max = sb.tile([P, 1], F32, name="neg_max%d" % h)
-            nc.vector.tensor_reduce(out=neg_max[:], in_=s[:], axis=mybir.AxisListType.X, op=ALU.max, negate=True)
-            p = sb.tile([P, I], F32, name="p%d" % h)
-            total = sb.tile([P, 1], F32, name="total%d" % h)
-            nc.scalar.activation(out=p[:], in_=s[:], func=ACT.Exp, bias=neg_max[:], accum_out=total[:])
-            probs.append(p)
-            sums.append(total)
+        size_ps = ps.tile([P, PACK, P], F32, name="size_ps")
+        for t in range(PACK):
+            nc.tensor.transpose(size_ps[:, t, :], size_raw[:, t:t + 1].to_broadcast([P, P]), ident[:])
 
-        def turn(name, rows_bf16, tag, bufs):
+        plane0_bf16 = sb.tile([P, T], BF16, name="plane0_bf16", align_bytes=64)
+        nc.scalar.activation(out=plane0_bf16[:], in_=val_planes[0][:], func=ACT.Copy)
+        v_g0 = sb.tile([P, I], BF16, name="v_g0", align_bytes=64)
+        nc.scalar.activation(out=v_g0[:], in_=plane0_bf16[:].indirect(slots[:]), func=ACT.Copy)
+
+        scores = [sb.tile([P, I], F32, name="s%d" % h) for h in range(HALVES)]
+        neg_max = [sb.tile([P, 1], F32, name="neg_max%d" % h) for h in range(HALVES)]
+        probs = [sb.tile([P, I], F32, name="p%d" % h) for h in range(HALVES)]
+        sums = [sb.tile([P, 1], F32, name="total%d" % h) for h in range(HALVES)]
+        inv = [sb.tile([P, 1], F32, name="inv%d" % h) for h in range(HALVES)]
+        for h in range(HALVES):
+            nc.vector.scalar_tensor_tensor(out=scores[h][:], in0=b_g[h][:], scalar=1.0, in1=a_ps[h][:], op0=ALU.add, op1=ALU.mult)
+        for h in range(HALVES):
+            nc.vector.tensor_reduce(out=neg_max[h][:], in_=scores[h][:], axis=mybir.AxisListType.X, op=ALU.max, negate=True)
+            nc.scalar.activation(out=probs[h][:], in_=scores[h][:], func=ACT.Exp, bias=neg_max[h][:], accum_out=sums[h][:])
+
+        def turn(name, rows_bf16, tag, bufs, grp):
             words = rows_bf16[:].bitcast(F32)
             bank = ps.tile([P, 2, P], F32, name=name + "_ps", tag=tag, bufs=bufs)
             for u in range(2):
                 nc.tensor.transpose(bank[:, u, :], words[:, u::2], ident[:])
-            grp = sb.tile([P, P, PACK], BF16, name=name + "_grp", align_bytes=64)
-            nc.scalar.copy(out=grp[:].rearrange("p c t -> p (c t)").bitcast(F32).rearrange("p (c u) -> p c u", u=2),
+            nc.scalar.copy(out=grp.rearrange("p c t -> p (c t)").bitcast(F32).rearrange("p (c u) -> p c u", u=2),
                            in_=bank[:].rearrange("p u c -> p c u"))
-            return grp
 
-        def gather_values(j):
+        wt_grp = sb.tile([P, Q, PACK], BF16, name="wt_grp", align_bytes=64)
+        vt01_grp = sb.tile([P, 2 * P, PACK], BF16, name="vt01_grp", align_bytes=64)
+        vt2_grp = sb.tile([P, P, PACK], BF16, name="vt2_grp", align_bytes=64)
+        vt3_grp = sb.tile([P, P, PACK], BF16, name="vt3_grp", align_bytes=64)
+
+        def gather_values(j, grp):
             v_g = sb.tile([P, I], BF16, name="v_g%d" % j, align_bytes=64)
             nc.vector.tensor_copy(v_g[:], val_planes[j][:].indirect(slots[:]))
-            return turn("vt%d" % j, v_g, "vt", 3)
+            turn("vt%d" % j, v_g, "vt", 3, grp)
 
         def weights(h):
-            inv = sb.tile([P, 1], F32, name="inv%d" % h)
-            nc.vector.reciprocal(out=inv[:], in_=sums[h][:])
             w = sb.tile([P, I], BF16, name="w%d" % h, align_bytes=64)
             nc.vector.scalar_tensor_tensor(out=w[:].rearrange("q (s t) -> q s t", t=PACK),
-                                           in0=probs[h][:].rearrange("q (s t) -> q s t", t=PACK), scalar=inv[:],
+                                           in0=probs[h][:].rearrange("q (s t) -> q s t", t=PACK), scalar=inv[h][:],
                                            in1=size_ps[:].rearrange("q t s -> q s t"), op0=ALU.mult, op1=ALU.mult)
-            return turn("wt%d" % h, w, "a_or_wt", 2)
-
-        wt_grp0 = weights(0)
-        vt_grp0 = gather_values(0)
-        wt_grp1 = weights(1)
-        vt_grp1 = gather_values(1)
-        wt_mx = [quantize("wt0", wt_grp0[:], P)]
-        vt_mx = [quantize("vt0", vt_grp0[:], P)]
-        wt_mx.append(quantize("wt1", wt_grp1[:], P))
-        vt_grp2 = gather_values(2)
-        vt_mx.append(quantize("vt1", vt_grp1[:], P))
-        vt_grp3 = gather_values(3)
-        vt_mx.append(quantize("vt2", vt_grp2[:], P))
-        vt_mx.append(quantize("vt3", vt_grp3[:], P))
+            turn("wt%d" % h, w, "a_or_wt", 2, wt_grp[:, h * P:(h + 1) * P, :])
 
         o_ps = [ps.tile([P, PACK, P], F32, name="o_ps%d" % h, tag="b_or_out", bufs=2) for h in range(HALVES)]
         o_sb = sb.tile([P, PACK, Q], F32, name="o_sb")
         out_rows = out_0.rearrange("(m j) q -> m j q", j=PACK)
 
-        def product(j):
+        def product(j, codes, scales):
             for h in range(HALVES):
-                nc.tensor.matmul_mx(out=o_ps[h][:, j, :], lhsT=vt_mx[j][0][:].bitcast(FP8X4), lhsT_scale=vt_mx[j][1][:],
-                                    rhs=wt_mx[h][0][:].bitcast(FP8X4), rhs_scale=wt_mx[h][1][:], start=True, stop=True)
+                cols = slice(h * P, (h + 1) * P)
+                nc.tensor.matmul_mx(out=o_ps[h][:, j, :], lhsT=codes.bitcast(FP8X4), lhsT_scale=scales,
+                                    rhs=wt_codes[:, cols].bitcast(FP8X4), rhs_scale=wt_scales[:, cols], start=True, stop=True)
 
-        last = PACK - 1
-        for j in range(last):
-            product(j)
+        turn("vt0", v_g0, "vt", 3, vt01_grp[:, :P, :])
+        gather_values(1, vt01_grp[:, P:, :])
         for h in range(HALVES):
-            nc.scalar.copy(out=o_sb[:, :last, h * P:(h + 1) * P], in_=o_ps[h][:, :last, :])
-        nc.sync.dma_start(out=out_rows[:, :last, :], in_=o_sb[:, :last, :])
-        product(last)
+            nc.vector.reciprocal(out=inv[h][:], in_=sums[h][:])
+        weights(0)
+        weights(1)
+        gather_values(2, vt2_grp[:])
+        wt_codes, wt_scales = quantize("wt", wt_grp[:], Q)
+        codes, scales = quantize("vt01", vt01_grp[:], 2 * P, after="plane2")
+        product(0, codes[:, :P], scales[:, :P])
+        product(1, codes[:, P:], scales[:, P:])
+        for h in range(HALVES):
+            nc.scalar.copy(out=o_sb[:, :2, h * P:(h + 1) * P], in_=o_ps[h][:, :2, :])
+        nc.sync.dma_start(out=out_rows[:, :2, :], in_=o_sb[:, :2, :])
+        gather_values(3, vt3_grp[:])
+        codes, scales = quantize("vt2", vt2_grp[:], P, after="plane3")
+        product(2, codes[:], scales[:])
+        codes, scales = quantize("vt3", vt3_grp[:], P)
+        product(3, codes[:], scales[:])
 
         o_grp = sb.tile([P, Q, PACK], BF16, name="o_grp", align_bytes=64)
         nc.vector.tensor_copy(out=o_grp[:, :P, :], in_=o_ps[0][:].rearrange("m j q -> m q j"))
         nc.scalar.copy(out=o_grp[:, P:, :], in_=o_ps[1][:].rearrange("m j q -> m q j"))
         for h in (1, 0):
-            nc.scalar.copy(out=o_sb[:, last, h * P:(h + 1) * P], in_=o_ps[h][:, last, :])
+            nc.scalar.copy(out=o_sb[:, 2:, h * P:(h + 1) * P], in_=o_ps[h][:, 2:, :])
         o_codes, o_scales = quantize("o", o_grp[:], Q)
-        nc.sync.dma_start(out=out_rows[:, last, :], in_=o_sb[:, last, :])
+        nc.scalar.dma_start(out=out_rows[:, 2:, :], in_=o_sb[:, 2:, :])
         nc.sync.dma_start(out=out_1[0].rearrange("l c r -> l (c r)").bitcast(I32), in_=o_codes[:].bitcast(I32))
         for quad in range(4):
             queue = nc.scalar if quad % 2 else nc.sync

@@ -53,19 +53,18 @@ def tile_attend_productscores_pl_kernel(tc, query, keys_words, keys_scales, pque
         warm_out = sb.tile([P, 8], F32, name="warm_out")
         nc.gpsimd.memset(warm[:], 0.0)
         nc.scalar.activation(out=warm_out[:], in_=warm[:], func=ACT.Exp)
-        nc.gpsimd.memset(key_scales[:].bitcast(I32), 0)
-        nc.sync.dma_start(slots[:], offs)
-        nc.sync.dma_start(places[:], offs2)
-        nc.sync.dma_start(out=size_raw[:], in_=size[0].rearrange("(p t) -> p t", t=PACK))
         nc.sync.dma_start(out=pq_raw[:], in_=pquery.rearrange("(p t) q -> p t q", t=PACK))
-        for quad in range(4):
-            nc.scalar.dma_start(out=key_scales[32 * quad:32 * quad + 4, :].bitcast(I32),
-                                in_=keys_scales[0, 4 * quad:4 * quad + 4, :].bitcast(I32))
+        nc.sync.dma_start(slots[:], offs)
         place_rows = place.rearrange("(p t) u -> p t u", t=PACK)
         for g in range(2):
             nc.sync.dma_start(out=place_raw[g][:], in_=place_rows[:, :, g * (U // 2):(g + 1) * (U // 2)])
+        for quad in range(4):
+            nc.sync.dma_start(out=key_scales[32 * quad:32 * quad + 32, :].bitcast(I32),
+                                in_=keys_scales[0, 4 * quad:4 * quad + 4, :].bitcast(I32).partition_broadcast(8))
         nc.sync.dma_start(out=key_words[:].bitcast(I32), in_=keys_words[0].bitcast(I32))
         nc.sync.dma_start(out=q_raw[:], in_=query.rearrange("(p t) q -> p t q", t=PACK))
+        nc.sync.dma_start(places[:], offs2)
+        nc.sync.dma_start(out=size_raw[:], in_=size[0].rearrange("(p t) -> p t", t=PACK))
         val_rows = vals.rearrange("(m j) t -> m j t", j=PACK)
         for j in range(PACK):
             nc.sync.dma_start(out=val_planes[j][:], in_=val_rows[:, j, :])
@@ -79,13 +78,13 @@ def tile_attend_productscores_pl_kernel(tc, query, keys_words, keys_scales, pque
         pq_grp = sb.tile([P, Q, PACK], BF16, name="pq_grp", align_bytes=64)
         interleave(nc.vector.tensor_copy, pq_grp[:], pq_raw[:])
         pq_codes, pq_scales = quantize("pq", pq_grp[:], Q)
-        ks_g = sb.tile([P, I], U8, name="ks_g", align_bytes=64)
-        nc.vector.tensor_copy(ks_g[:], key_scales[:].indirect(slots[:]))
         place_grp = [sb.tile([P, U // 2, PACK], BF16, name="place_grp%d" % g, align_bytes=64) for g in range(2)]
         interleave(nc.scalar.copy, place_grp[0][:], place_raw[0][:])
         interleave(nc.vector.tensor_copy, place_grp[1][:], place_raw[1][:])
         place_mx = [quantize("place%d" % g, place_grp[g][:], U // 2) for g in range(2)]
 
+        ks_g = sb.tile([P, I], U8, name="ks_g", align_bytes=64)
+        nc.vector.tensor_copy(ks_g[:], key_scales[:].indirect(slots[:]))
         kw_g = sb.tile([P, I], U16, name="kw_g", align_bytes=64)
         nc.vector.tensor_copy(kw_g[:], key_words[:].indirect(slots[:]))
 
@@ -100,17 +99,21 @@ def tile_attend_productscores_pl_kernel(tc, query, keys_words, keys_scales, pque
                                     start=True, stop=True)
             b_ps.append(bank)
 
-        a_ps, b_g = [], []
         for h in range(HALVES):
             nc.scalar.copy(out=b_sb[h][:, :U], in_=b_ps[h][:])
-            gathered = sb.tile([P, I], F32, name="b_g%d" % h)
-            nc.vector.tensor_copy(gathered[:], b_sb[h][:].indirect(places[:]))
-            b_g.append(gathered)
-            grp = sb.tile([P, P, PACK], BF16, name="q_grp%d" % h, align_bytes=64)
-            interleave(nc.scalar.copy, grp[:], q_raw[:, :, h * P:(h + 1) * P])
-            codes, scales = quantize("q%d" % h, grp[:], P)
+        q_grp = sb.tile([P, Q, PACK], BF16, name="q_grp", tag="q_grp", align_bytes=64)
+        interleave(nc.scalar.copy, q_grp[:], q_raw[:])
+        b_g0 = sb.tile([P, I], F32, name="b_g0", align_bytes=64)
+        nc.vector.tensor_copy(b_g0[:], b_sb[0][:].indirect(places[:]))
+        q_codes, q_scales = quantize("q", q_grp[:], Q)
+        b_g1 = sb.tile([P, I], F32, name="b_g1", tag="q_grp", align_bytes=64)
+        nc.vector.tensor_copy(b_g1[:], b_sb[1][:].indirect(places[:]))
+        b_g = [b_g0, b_g1]
+        a_ps = []
+        for h in range(HALVES):
+            cols = slice(h * P, (h + 1) * P)
             bank = ps.tile([P, I], F32, name="a_ps%d" % h, tag="a_or_wt", bufs=2)
-            nc.tensor.matmul_mx(out=bank[:], lhsT=codes[:].bitcast(FP8X4), lhsT_scale=scales[:],
+            nc.tensor.matmul_mx(out=bank[:], lhsT=q_codes[:, cols].bitcast(FP8X4), lhsT_scale=q_scales[:, cols],
                                 rhs=kw_g[:].bitcast(FP4X4), rhs_scale=ks_g[:], start=True, stop=True)
             a_ps.append(bank)
 
@@ -120,19 +123,20 @@ def tile_attend_productscores_pl_kernel(tc, query, keys_words, keys_scales, pque
 
         plane0_bf16 = sb.tile([P, T], BF16, name="plane0_bf16", align_bytes=64)
         nc.scalar.activation(out=plane0_bf16[:], in_=val_planes[0][:], func=ACT.Copy)
-        v_g0 = sb.tile([P, I], BF16, name="v_g0", align_bytes=64)
-        nc.scalar.activation(out=v_g0[:], in_=plane0_bf16[:].indirect(slots[:]), func=ACT.Copy)
 
-        scores = [sb.tile([P, I], F32, name="s%d" % h) for h in range(HALVES)]
+        scores = [sb.tile([P, I], F32, name="s%d" % h, tag="s%d" % h, align_bytes=64) for h in range(HALVES)]
         neg_max = [sb.tile([P, 1], F32, name="neg_max%d" % h) for h in range(HALVES)]
         probs = [sb.tile([P, I], F32, name="p%d" % h) for h in range(HALVES)]
-        sums = [sb.tile([P, 1], F32, name="total%d" % h) for h in range(HALVES)]
-        inv = [sb.tile([P, 1], F32, name="inv%d" % h) for h in range(HALVES)]
+        sums = sb.tile([P, HALVES], F32, name="sums")
+        inv = sb.tile([P, HALVES], F32, name="inv")
         for h in range(HALVES):
             nc.vector.scalar_tensor_tensor(out=scores[h][:], in0=b_g[h][:], scalar=1.0, in1=a_ps[h][:], op0=ALU.add, op1=ALU.mult)
         for h in range(HALVES):
             nc.vector.tensor_reduce(out=neg_max[h][:], in_=scores[h][:], axis=mybir.AxisListType.X, op=ALU.max, negate=True)
-            nc.scalar.activation(out=probs[h][:], in_=scores[h][:], func=ACT.Exp, bias=neg_max[h][:], accum_out=sums[h][:])
+            nc.scalar.activation(out=probs[h][:], in_=scores[h][:], func=ACT.Exp, bias=neg_max[h][:], accum_out=sums[:, h:h + 1])
+
+        v_g0 = sb.tile([P, I], BF16, name="v_g0", tag="s1", align_bytes=64)
+        nc.scalar.activation(out=v_g0[:], in_=plane0_bf16[:].indirect(slots[:]), func=ACT.Copy)
 
         def turn(name, rows_bf16, tag, bufs, grp):
             words = rows_bf16[:].bitcast(F32)
@@ -142,20 +146,21 @@ def tile_attend_productscores_pl_kernel(tc, query, keys_words, keys_scales, pque
             nc.scalar.copy(out=grp.rearrange("p c t -> p (c t)").bitcast(F32).rearrange("p (c u) -> p c u", u=2),
                            in_=bank[:].rearrange("p u c -> p c u"))
 
-        wt_grp = sb.tile([P, Q, PACK], BF16, name="wt_grp", align_bytes=64)
-        vt01_grp = sb.tile([P, 2 * P, PACK], BF16, name="vt01_grp", align_bytes=64)
+        joint_grp = sb.tile([P, Q + 2 * P, PACK], BF16, name="joint_grp", tag="joint_grp", align_bytes=64)
+        wt_grp = joint_grp[:, :Q, :]
+        vt01_grp = joint_grp[:, Q:, :]
         vt2_grp = sb.tile([P, P, PACK], BF16, name="vt2_grp", align_bytes=64)
         vt3_grp = sb.tile([P, P, PACK], BF16, name="vt3_grp", align_bytes=64)
 
-        def gather_values(j, grp):
-            v_g = sb.tile([P, I], BF16, name="v_g%d" % j, align_bytes=64)
+        def gather_values(j, grp, tag):
+            v_g = sb.tile([P, I], BF16, name="v_g%d" % j, tag=tag, align_bytes=64)
             nc.vector.tensor_copy(v_g[:], val_planes[j][:].indirect(slots[:]))
             turn("vt%d" % j, v_g, "vt", 3, grp)
 
         def weights(h):
             w = sb.tile([P, I], BF16, name="w%d" % h, align_bytes=64)
             nc.vector.scalar_tensor_tensor(out=w[:].rearrange("q (s t) -> q s t", t=PACK),
-                                           in0=probs[h][:].rearrange("q (s t) -> q s t", t=PACK), scalar=inv[h][:],
+                                           in0=probs[h][:].rearrange("q (s t) -> q s t", t=PACK), scalar=inv[:, h:h + 1],
                                            in1=size_ps[:].rearrange("q t s -> q s t"), op0=ALU.mult, op1=ALU.mult)
             turn("wt%d" % h, w, "a_or_wt", 2, wt_grp[:, h * P:(h + 1) * P, :])
 
@@ -169,21 +174,19 @@ def tile_attend_productscores_pl_kernel(tc, query, keys_words, keys_scales, pque
                 nc.tensor.matmul_mx(out=o_ps[h][:, j, :], lhsT=codes.bitcast(FP8X4), lhsT_scale=scales,
                                     rhs=wt_codes[:, cols].bitcast(FP8X4), rhs_scale=wt_scales[:, cols], start=True, stop=True)
 
+        gather_values(1, vt01_grp[:, P:, :], "v_g1")
         turn("vt0", v_g0, "vt", 3, vt01_grp[:, :P, :])
-        gather_values(1, vt01_grp[:, P:, :])
-        for h in range(HALVES):
-            nc.vector.reciprocal(out=inv[h][:], in_=sums[h][:])
+        nc.vector.reciprocal(out=inv[:], in_=sums[:])
         weights(0)
         weights(1)
-        gather_values(2, vt2_grp[:])
-        wt_codes, wt_scales = quantize("wt", wt_grp[:], Q)
-        codes, scales = quantize("vt01", vt01_grp[:], 2 * P, after="plane2")
-        product(0, codes[:, :P], scales[:, :P])
-        product(1, codes[:, P:], scales[:, P:])
+        gather_values(2, vt2_grp[:], "v_g2")
+        wt_codes, wt_scales = quantize("joint", joint_grp[:], Q + 2 * P)
+        product(0, wt_codes[:, Q:Q + P], wt_scales[:, Q:Q + P])
+        product(1, wt_codes[:, Q + P:], wt_scales[:, Q + P:])
         for h in range(HALVES):
             nc.scalar.copy(out=o_sb[:, :2, h * P:(h + 1) * P], in_=o_ps[h][:, :2, :])
         nc.sync.dma_start(out=out_rows[:, :2, :], in_=o_sb[:, :2, :])
-        gather_values(3, vt3_grp[:])
+        gather_values(3, vt3_grp[:], "joint_grp")
         codes, scales = quantize("vt2", vt2_grp[:], P, after="plane3")
         product(2, codes[:], scales[:])
         codes, scales = quantize("vt3", vt3_grp[:], P)
@@ -194,7 +197,12 @@ def tile_attend_productscores_pl_kernel(tc, query, keys_words, keys_scales, pque
         nc.scalar.copy(out=o_grp[:, P:, :], in_=o_ps[1][:].rearrange("m j q -> m q j"))
         for h in (1, 0):
             nc.scalar.copy(out=o_sb[:, 2:, h * P:(h + 1) * P], in_=o_ps[h][:, 2:, :])
-        o_codes, o_scales = quantize("o", o_grp[:], Q)
+        o_codes = sb.tile([P, Q], U32, name="o_codes", align_bytes=64)
+        o_scales = sb.tile([P, Q], U8, name="o_scales", align_bytes=64)
+        for h in (1, 0):
+            cols = slice(h * P, (h + 1) * P)
+            nc.vector.quantize_mx(out=o_codes[:, cols].bitcast(FP8X4), scales=o_scales[:, cols],
+                                  in_=o_grp[:, cols, :].rearrange("p c t -> p (c t)"))
         nc.scalar.dma_start(out=out_rows[:, 2:, :], in_=o_sb[:, 2:, :])
         nc.sync.dma_start(out=out_1[0].rearrange("l c r -> l (c r)").bitcast(I32), in_=o_codes[:].bitcast(I32))
         for quad in range(4):

@@ -19,8 +19,12 @@ ACT = mybir.ActivationFunctionType
 
 P = 128
 PACK = 4
+QUADRANT = 32
 HALVES = Q // P
+U_PART = U // 2
 B_WINDOW = 704
+PLACE_ON_VECTOR = 192
+OUT_ON_VECTOR = 176
 
 
 def tile_attend_productscores_pl_kernel(tc, query, keys_words, keys_scales, pquery, place, size, vals, offs, offs2,
@@ -30,11 +34,14 @@ def tile_attend_productscores_pl_kernel(tc, query, keys_words, keys_scales, pque
         sb = ctx.enter_context(tc.tile_pool(name="sb", bufs=1))
         ps = ctx.enter_context(tc.psum_pool(name="ps", bufs=1))
 
-        def interleave(engine_copy, dst, src):
-            engine_copy(out=dst.rearrange("p (c i) t -> p c t i", i=4), in_=src.rearrange("p t (c i) -> p c t i", i=4))
+        def scalar_cast(out, in_):
+            nc.scalar.activation(out=out, in_=in_, func=ACT.Copy)
 
-        def quantize(name, grouped, width, after=None):
-            codes = sb.tile([P, width], U32, name=name + "_codes", align_bytes=64, tag=after or name + "_codes")
+        def group(copy, grouped, rows):
+            copy(out=grouped.rearrange("p (c i) t -> p c t i", i=4), in_=rows.rearrange("p t (c i) -> p c t i", i=4))
+
+        def quantize(name, grouped, width, codes_tag=None):
+            codes = sb.tile([P, width], U32, name=name + "_codes", align_bytes=64, tag=codes_tag or name + "_codes")
             scales = sb.tile([P, width], U8, name=name + "_scales", align_bytes=64)
             nc.vector.quantize_mx(out=codes[:].bitcast(FP8X4), scales=scales[:], in_=grouped.rearrange("p c t -> p (c t)"))
             return codes, scales
@@ -45,29 +52,26 @@ def tile_attend_productscores_pl_kernel(tc, query, keys_words, keys_scales, pque
         key_words = sb.tile([P, T], U16, name="key_words", align_bytes=64)
         pq_raw = sb.tile([P, PACK, Q], F32, name="pq_raw")
         q_raw = sb.tile([P, PACK, Q], F32, name="q_raw")
-        place_raw = [sb.tile([P, PACK, U // 2], F32, name="place_raw%d" % g) for g in range(2)]
+        place_raw = [sb.tile([P, PACK, U_PART], F32, name="place_raw%d" % g) for g in range(2)]
         size_raw = sb.tile([P, PACK], F32, name="size_raw")
-        val_planes = [sb.tile([P, T], F32, name="val_plane%d" % j, tag="plane%d" % j, align_bytes=64) for j in range(PACK)]
+        planes = [sb.tile([P, T], F32, name="plane%d" % j, tag="plane%d" % j, align_bytes=64) for j in range(PACK)]
 
-        warm = sb.tile([P, 8], F32, name="warm")
-        warm_out = sb.tile([P, 8], F32, name="warm_out")
-        nc.gpsimd.memset(warm[:], 0.0)
-        nc.scalar.activation(out=warm_out[:], in_=warm[:], func=ACT.Exp)
         nc.sync.dma_start(out=pq_raw[:], in_=pquery.rearrange("(p t) q -> p t q", t=PACK))
         nc.sync.dma_start(slots[:], offs)
         place_rows = place.rearrange("(p t) u -> p t u", t=PACK)
         for g in range(2):
-            nc.sync.dma_start(out=place_raw[g][:], in_=place_rows[:, :, g * (U // 2):(g + 1) * (U // 2)])
-        for quad in range(4):
-            nc.sync.dma_start(out=key_scales[32 * quad:32 * quad + 32, :].bitcast(I32),
-                                in_=keys_scales[0, 4 * quad:4 * quad + 4, :].bitcast(I32).partition_broadcast(8))
+            nc.sync.dma_start(out=place_raw[g][:], in_=place_rows[:, :, g * U_PART:(g + 1) * U_PART])
+        for quad in range(P // QUADRANT):
+            nc.sync.dma_start(out=key_scales[QUADRANT * quad:QUADRANT * (quad + 1), :].bitcast(I32),
+                              in_=keys_scales[0, PACK * quad:PACK * (quad + 1), :].bitcast(I32)
+                              .partition_broadcast(QUADRANT // PACK))
         nc.sync.dma_start(out=key_words[:].bitcast(I32), in_=keys_words[0].bitcast(I32))
         nc.sync.dma_start(out=q_raw[:], in_=query.rearrange("(p t) q -> p t q", t=PACK))
         nc.sync.dma_start(places[:], offs2)
         nc.sync.dma_start(out=size_raw[:], in_=size[0].rearrange("(p t) -> p t", t=PACK))
         val_rows = vals.rearrange("(m j) t -> m j t", j=PACK)
         for j in range(PACK):
-            nc.sync.dma_start(out=val_planes[j][:], in_=val_rows[:, j, :])
+            nc.sync.dma_start(out=planes[j][:], in_=val_rows[:, j, :])
 
         ident = sb.tile([P, P], F32, name="ident")
         make_identity(nc, ident[:])
@@ -76,45 +80,46 @@ def tile_attend_productscores_pl_kernel(tc, query, keys_words, keys_scales, pque
             nc.gpsimd.memset(b_sb[h][:, U:], 0.0)
 
         pq_grp = sb.tile([P, Q, PACK], BF16, name="pq_grp", align_bytes=64)
-        interleave(nc.vector.tensor_copy, pq_grp[:], pq_raw[:])
+        group(nc.vector.tensor_copy, pq_grp[:], pq_raw[:])
         pq_codes, pq_scales = quantize("pq", pq_grp[:], Q)
-        place_grp = [sb.tile([P, U // 2, PACK], BF16, name="place_grp%d" % g, align_bytes=64) for g in range(2)]
-        interleave(nc.scalar.copy, place_grp[0][:], place_raw[0][:])
-        interleave(nc.vector.tensor_copy, place_grp[1][:], place_raw[1][:])
-        place_mx = [quantize("place%d" % g, place_grp[g][:], U // 2) for g in range(2)]
+        place_grp = [sb.tile([P, U_PART, PACK], BF16, name="place_grp%d" % g, align_bytes=64) for g in range(2)]
+        group(nc.vector.tensor_copy, place_grp[0][:], place_raw[0][:])
+        group(nc.vector.tensor_copy, place_grp[1][:, :PLACE_ON_VECTOR, :], place_raw[1][:, :, :PLACE_ON_VECTOR])
+        group(scalar_cast, place_grp[1][:, PLACE_ON_VECTOR:, :], place_raw[1][:, :, PLACE_ON_VECTOR:])
+        place_mx = [quantize("place%d" % g, place_grp[g][:], U_PART) for g in range(2)]
 
-        ks_g = sb.tile([P, I], U8, name="ks_g", align_bytes=64)
-        nc.vector.tensor_copy(ks_g[:], key_scales[:].indirect(slots[:]))
-        kw_g = sb.tile([P, I], U16, name="kw_g", align_bytes=64)
-        nc.vector.tensor_copy(kw_g[:], key_words[:].indirect(slots[:]))
+        slot_scales = sb.tile([P, I], U8, name="slot_scales", align_bytes=64)
+        nc.vector.tensor_copy(slot_scales[:], key_scales[:].indirect(slots[:]))
+        slot_words = sb.tile([P, I], U16, name="slot_words", align_bytes=64)
+        nc.vector.tensor_copy(slot_words[:], key_words[:].indirect(slots[:]))
 
         b_ps = []
         for h in range(HALVES):
             cols = slice(h * P, (h + 1) * P)
-            bank = ps.tile([P, U], F32, name="b_ps%d" % h, tag="b_or_out", bufs=2)
+            bank = ps.tile([P, U], F32, name="b_ps%d" % h, tag="b_then_out", bufs=2)
             for g in range(2):
-                nc.tensor.matmul_mx(out=bank[:, g * (U // 2):(g + 1) * (U // 2)],
+                nc.tensor.matmul_mx(out=bank[:, g * U_PART:(g + 1) * U_PART],
                                     lhsT=pq_codes[:, cols].bitcast(FP8X4), lhsT_scale=pq_scales[:, cols],
                                     rhs=place_mx[g][0][:].bitcast(FP8X4), rhs_scale=place_mx[g][1][:],
                                     start=True, stop=True)
             b_ps.append(bank)
-
         for h in range(HALVES):
             nc.scalar.copy(out=b_sb[h][:, :U], in_=b_ps[h][:])
+
         q_grp = sb.tile([P, Q, PACK], BF16, name="q_grp", tag="q_grp", align_bytes=64)
-        interleave(nc.scalar.copy, q_grp[:], q_raw[:])
-        b_g0 = sb.tile([P, I], F32, name="b_g0", align_bytes=64)
-        nc.vector.tensor_copy(b_g0[:], b_sb[0][:].indirect(places[:]))
+        group(nc.scalar.copy, q_grp[:], q_raw[:])
+        b_slots0 = sb.tile([P, I], F32, name="b_slots0", align_bytes=64)
+        nc.vector.tensor_copy(b_slots0[:], b_sb[0][:].indirect(places[:]))
         q_codes, q_scales = quantize("q", q_grp[:], Q)
-        b_g1 = sb.tile([P, I], F32, name="b_g1", tag="q_grp", align_bytes=64)
-        nc.vector.tensor_copy(b_g1[:], b_sb[1][:].indirect(places[:]))
-        b_g = [b_g0, b_g1]
+        b_slots1 = sb.tile([P, I], F32, name="b_slots1", tag="q_grp", align_bytes=64)
+        nc.vector.tensor_copy(b_slots1[:], b_sb[1][:].indirect(places[:]))
+        b_slots = [b_slots0, b_slots1]
         a_ps = []
         for h in range(HALVES):
             cols = slice(h * P, (h + 1) * P)
-            bank = ps.tile([P, I], F32, name="a_ps%d" % h, tag="a_or_wt", bufs=2)
+            bank = ps.tile([P, I], F32, name="a_ps%d" % h, tag="a_then_wt", bufs=2)
             nc.tensor.matmul_mx(out=bank[:], lhsT=q_codes[:, cols].bitcast(FP8X4), lhsT_scale=q_scales[:, cols],
-                                rhs=kw_g[:].bitcast(FP4X4), rhs_scale=ks_g[:], start=True, stop=True)
+                                rhs=slot_words[:].bitcast(FP4X4), rhs_scale=slot_scales[:], start=True, stop=True)
             a_ps.append(bank)
 
         size_ps = ps.tile([P, PACK, P], F32, name="size_ps")
@@ -122,90 +127,89 @@ def tile_attend_productscores_pl_kernel(tc, query, keys_words, keys_scales, pque
             nc.tensor.transpose(size_ps[:, t, :], size_raw[:, t:t + 1].to_broadcast([P, P]), ident[:])
 
         plane0_bf16 = sb.tile([P, T], BF16, name="plane0_bf16", align_bytes=64)
-        nc.scalar.activation(out=plane0_bf16[:], in_=val_planes[0][:], func=ACT.Copy)
+        scalar_cast(plane0_bf16[:], planes[0][:])
 
         scores = [sb.tile([P, I], F32, name="s%d" % h, tag="s%d" % h, align_bytes=64) for h in range(HALVES)]
         neg_max = [sb.tile([P, 1], F32, name="neg_max%d" % h) for h in range(HALVES)]
-        probs = [sb.tile([P, I], F32, name="p%d" % h) for h in range(HALVES)]
+        probs = [sb.tile([P, I], F32, name="p0", tag="plane0", align_bytes=64), sb.tile([P, I], F32, name="p1")]
         sums = sb.tile([P, HALVES], F32, name="sums")
-        inv = sb.tile([P, HALVES], F32, name="inv")
+        inv_sums = sb.tile([P, HALVES], F32, name="inv_sums")
         for h in range(HALVES):
-            nc.vector.scalar_tensor_tensor(out=scores[h][:], in0=b_g[h][:], scalar=1.0, in1=a_ps[h][:], op0=ALU.add, op1=ALU.mult)
+            nc.vector.scalar_tensor_tensor(out=scores[h][:], in0=b_slots[h][:], scalar=1.0, in1=a_ps[h][:],
+                                           op0=ALU.add, op1=ALU.mult)
         for h in range(HALVES):
             nc.vector.tensor_reduce(out=neg_max[h][:], in_=scores[h][:], axis=mybir.AxisListType.X, op=ALU.max, negate=True)
-            nc.scalar.activation(out=probs[h][:], in_=scores[h][:], func=ACT.Exp, bias=neg_max[h][:], accum_out=sums[:, h:h + 1])
+            nc.scalar.activation(out=probs[h][:], in_=scores[h][:], func=ACT.Exp, bias=neg_max[h][:],
+                                 accum_out=sums[:, h:h + 1])
 
-        v_g0 = sb.tile([P, I], BF16, name="v_g0", tag="s1", align_bytes=64)
-        nc.scalar.activation(out=v_g0[:], in_=plane0_bf16[:].indirect(slots[:]), func=ACT.Copy)
+        v_slots0 = sb.tile([P, I], BF16, name="v_slots0", tag="s1", align_bytes=64)
+        scalar_cast(v_slots0[:], plane0_bf16[:].indirect(slots[:]))
 
-        def turn(name, rows_bf16, tag, bufs, grp):
-            words = rows_bf16[:].bitcast(F32)
+        def turn(name, by_slot, tag, bufs, grouped):
+            words = by_slot[:].bitcast(F32)
             bank = ps.tile([P, 2, P], F32, name=name + "_ps", tag=tag, bufs=bufs)
             for u in range(2):
                 nc.tensor.transpose(bank[:, u, :], words[:, u::2], ident[:])
-            nc.scalar.copy(out=grp.rearrange("p c t -> p (c t)").bitcast(F32).rearrange("p (c u) -> p c u", u=2),
+            nc.scalar.copy(out=grouped.rearrange("p c t -> p (c t)").bitcast(F32).rearrange("p (c u) -> p c u", u=2),
                            in_=bank[:].rearrange("p u c -> p c u"))
 
         joint_grp = sb.tile([P, Q + 2 * P, PACK], BF16, name="joint_grp", tag="joint_grp", align_bytes=64)
-        wt_grp = joint_grp[:, :Q, :]
-        vt01_grp = joint_grp[:, Q:, :]
         vt2_grp = sb.tile([P, P, PACK], BF16, name="vt2_grp", align_bytes=64)
         vt3_grp = sb.tile([P, P, PACK], BF16, name="vt3_grp", align_bytes=64)
+        vt_banks = 3
 
-        def gather_values(j, grp, tag):
-            v_g = sb.tile([P, I], BF16, name="v_g%d" % j, tag=tag, align_bytes=64)
-            nc.vector.tensor_copy(v_g[:], val_planes[j][:].indirect(slots[:]))
-            turn("vt%d" % j, v_g, "vt", 3, grp)
+        def gather_values(j, grouped):
+            v_slots = sb.tile([P, I], BF16, name="v_slots%d" % j, align_bytes=64)
+            nc.vector.tensor_copy(v_slots[:], planes[j][:].indirect(slots[:]))
+            turn("vt%d" % j, v_slots, "vt", vt_banks, grouped)
 
         def weights(h):
             w = sb.tile([P, I], BF16, name="w%d" % h, align_bytes=64)
             nc.vector.scalar_tensor_tensor(out=w[:].rearrange("q (s t) -> q s t", t=PACK),
-                                           in0=probs[h][:].rearrange("q (s t) -> q s t", t=PACK), scalar=inv[:, h:h + 1],
+                                           in0=probs[h][:].rearrange("q (s t) -> q s t", t=PACK),
+                                           scalar=inv_sums[:, h:h + 1],
                                            in1=size_ps[:].rearrange("q t s -> q s t"), op0=ALU.mult, op1=ALU.mult)
-            turn("wt%d" % h, w, "a_or_wt", 2, wt_grp[:, h * P:(h + 1) * P, :])
+            turn("wt%d" % h, w, "a_then_wt", 2, joint_grp[:, h * P:(h + 1) * P, :])
 
-        o_ps = [ps.tile([P, PACK, P], F32, name="o_ps%d" % h, tag="b_or_out", bufs=2) for h in range(HALVES)]
-        o_sb = sb.tile([P, PACK, Q], F32, name="o_sb")
-        out_rows = out_0.rearrange("(m j) q -> m j q", j=PACK)
-
-        def product(j, codes, scales):
-            for h in range(HALVES):
-                cols = slice(h * P, (h + 1) * P)
-                nc.tensor.matmul_mx(out=o_ps[h][:, j, :], lhsT=codes.bitcast(FP8X4), lhsT_scale=scales,
-                                    rhs=wt_codes[:, cols].bitcast(FP8X4), rhs_scale=wt_scales[:, cols], start=True, stop=True)
-
-        gather_values(1, vt01_grp[:, P:, :], "v_g1")
-        turn("vt0", v_g0, "vt", 3, vt01_grp[:, :P, :])
-        nc.vector.reciprocal(out=inv[:], in_=sums[:])
+        gather_values(1, joint_grp[:, Q + P:, :])
+        turn("vt0", v_slots0, "vt", vt_banks, joint_grp[:, Q:Q + P, :])
+        nc.vector.reciprocal(out=inv_sums[:], in_=sums[:])
         weights(0)
         weights(1)
-        gather_values(2, vt2_grp[:], "v_g2")
-        wt_codes, wt_scales = quantize("joint", joint_grp[:], Q + 2 * P)
-        product(0, wt_codes[:, Q:Q + P], wt_scales[:, Q:Q + P])
-        product(1, wt_codes[:, Q + P:], wt_scales[:, Q + P:])
-        for h in range(HALVES):
-            nc.scalar.copy(out=o_sb[:, :2, h * P:(h + 1) * P], in_=o_ps[h][:, :2, :])
+        gather_values(2, vt2_grp[:])
+        gather_values(3, vt3_grp[:])
+        joint_codes, joint_scales = quantize("joint", joint_grp[:], Q + 2 * P, codes_tag="plane3")
+        vt2_codes, vt2_scales = quantize("vt2", vt2_grp[:], P, codes_tag="joint_grp")
+        vt3_codes, vt3_scales = quantize("vt3", vt3_grp[:], P)
+        vt_mx = [(joint_codes[:, Q:Q + P], joint_scales[:, Q:Q + P]), (joint_codes[:, Q + P:], joint_scales[:, Q + P:]),
+                 (vt2_codes[:], vt2_scales[:]), (vt3_codes[:], vt3_scales[:])]
+
+        o01_ps = ps.tile([P, 2, Q], F32, name="o01_ps", tag="b_then_out", bufs=2)
+        o2_ps = ps.tile([P, Q], F32, name="o2_ps", tag="b_then_out", bufs=2)
+        o3_ps = ps.tile([P, Q], F32, name="o3_ps", tag="a_then_wt", bufs=2)
+        for j, target in enumerate((o01_ps[:, 0, :], o01_ps[:, 1, :], o2_ps[:], o3_ps[:])):
+            nc.tensor.matmul_mx(out=target, lhsT=vt_mx[j][0].bitcast(FP8X4), lhsT_scale=vt_mx[j][1],
+                                rhs=joint_codes[:, :Q].bitcast(FP8X4), rhs_scale=joint_scales[:, :Q],
+                                start=True, stop=True)
+        out_rows = out_0.rearrange("(m j) q -> m j q", j=PACK)
+        o_sb = sb.tile([P, PACK, Q], F32, name="o_sb")
+        nc.scalar.copy(out=o_sb[:, :2, :], in_=o01_ps[:])
         nc.sync.dma_start(out=out_rows[:, :2, :], in_=o_sb[:, :2, :])
-        gather_values(3, vt3_grp[:], "joint_grp")
-        codes, scales = quantize("vt2", vt2_grp[:], P, after="plane3")
-        product(2, codes[:], scales[:])
-        codes, scales = quantize("vt3", vt3_grp[:], P)
-        product(3, codes[:], scales[:])
+        nc.vector.tensor_copy(out=o_sb[:, 2, :], in_=o2_ps[:])
+        nc.scalar.copy(out=o_sb[:, 3, :], in_=o3_ps[:])
+        nc.sync.dma_start(out=out_rows[:, 2:, :], in_=o_sb[:, 2:, :])
 
         o_grp = sb.tile([P, Q, PACK], BF16, name="o_grp", align_bytes=64)
-        nc.vector.tensor_copy(out=o_grp[:, :P, :], in_=o_ps[0][:].rearrange("m j q -> m q j"))
-        nc.scalar.copy(out=o_grp[:, P:, :], in_=o_ps[1][:].rearrange("m j q -> m q j"))
-        for h in (1, 0):
-            nc.scalar.copy(out=o_sb[:, 2:, h * P:(h + 1) * P], in_=o_ps[h][:, 2:, :])
+        group(nc.vector.tensor_copy, o_grp[:, :P, :], o_sb[:, :, :P])
+        group(nc.vector.tensor_copy, o_grp[:, P:OUT_ON_VECTOR, :], o_sb[:, :, P:OUT_ON_VECTOR])
+        group(nc.scalar.copy, o_grp[:, OUT_ON_VECTOR:, :], o_sb[:, :, OUT_ON_VECTOR:])
         o_codes = sb.tile([P, Q], U32, name="o_codes", align_bytes=64)
         o_scales = sb.tile([P, Q], U8, name="o_scales", align_bytes=64)
-        for h in (1, 0):
+        for h in range(HALVES):
             cols = slice(h * P, (h + 1) * P)
             nc.vector.quantize_mx(out=o_codes[:, cols].bitcast(FP8X4), scales=o_scales[:, cols],
                                   in_=o_grp[:, cols, :].rearrange("p c t -> p (c t)"))
-        nc.scalar.dma_start(out=out_rows[:, 2:, :], in_=o_sb[:, 2:, :])
         nc.sync.dma_start(out=out_1[0].rearrange("l c r -> l (c r)").bitcast(I32), in_=o_codes[:].bitcast(I32))
-        for quad in range(4):
-            queue = nc.scalar if quad % 2 else nc.sync
-            queue.dma_start(out=out_2[0, 4 * quad:4 * quad + 4, :].bitcast(I32),
-                            in_=o_scales[32 * quad:32 * quad + 4, :].bitcast(I32))
+        for quad, queue in enumerate((nc.sync, nc.sync, nc.scalar, nc.scalar)):
+            queue.dma_start(out=out_2[0, PACK * quad:PACK * (quad + 1), :].bitcast(I32),
+                            in_=o_scales[QUADRANT * quad:QUADRANT * quad + PACK, :].bitcast(I32))

from contextlib import ExitStack

import concourse.mybir as mybir
from concourse.masks import make_identity

D, T, I, Q, E, U = 512, 2048, 512, 256, 512, 512
FLOPS = 2 * D * Q * I + 2 * D * Q * U + 2 * I * E * Q

F32 = mybir.dt.float32
BF16 = mybir.dt.bfloat16
I32 = mybir.dt.int32
U32 = mybir.dt.uint32
U16 = mybir.dt.uint16
U8 = mybir.dt.uint8
FP8X4 = mybir.dt.float8_e4m3fn_x4
FP4X4 = mybir.dt.float4_e2m1fn_x4
ALU = mybir.AluOpType
ACT = mybir.ActivationFunctionType

P = 128
PACK = 4
QUADRANT = 32
HALVES = Q // P
U_PART = U // 2
B_WINDOW = 704
PLACE_ON_VECTOR = 192
OUT_ON_VECTOR = 176


def tile_attend_productscores_pl_kernel(tc, query, keys_words, keys_scales, pquery, place, size, vals, offs, offs2,
                                         out_0, out_1, out_2):
    nc = tc.nc
    with ExitStack() as ctx:
        sb = ctx.enter_context(tc.tile_pool(name="sb", bufs=1))
        ps = ctx.enter_context(tc.psum_pool(name="ps", bufs=1))

        def scalar_cast(out, in_):
            nc.scalar.activation(out=out, in_=in_, func=ACT.Copy)

        def group(copy, grouped, rows):
            copy(out=grouped.rearrange("p (c i) t -> p c t i", i=4), in_=rows.rearrange("p t (c i) -> p c t i", i=4))

        def quantize(name, grouped, width, codes_tag=None):
            codes = sb.tile([P, width], U32, name=name + "_codes", align_bytes=64, tag=codes_tag or name + "_codes")
            scales = sb.tile([P, width], U8, name=name + "_scales", align_bytes=64)
            nc.vector.quantize_mx(out=codes[:].bitcast(FP8X4), scales=scales[:], in_=grouped.rearrange("p c t -> p (c t)"))
            return codes, scales

        slots = sb.tile([P, I // 16], U16, name="slots")
        places = sb.tile([P, I // 16], U16, name="places")
        key_scales = sb.tile([P, T], U8, name="key_scales", align_bytes=64)
        key_words = sb.tile([P, T], U16, name="key_words", align_bytes=64)
        pq_raw = sb.tile([P, PACK, Q], F32, name="pq_raw")
        q_raw = sb.tile([P, PACK, Q], F32, name="q_raw")
        place_raw = [sb.tile([P, PACK, U_PART], F32, name="place_raw%d" % g) for g in range(2)]
        size_raw = sb.tile([P, PACK], F32, name="size_raw")
        planes = [sb.tile([P, T], F32, name="plane%d" % j, tag="plane%d" % j, align_bytes=64) for j in range(PACK)]

        nc.sync.dma_start(out=pq_raw[:], in_=pquery.rearrange("(p t) q -> p t q", t=PACK))
        nc.sync.dma_start(slots[:], offs)
        place_rows = place.rearrange("(p t) u -> p t u", t=PACK)
        for g in range(2):
            nc.sync.dma_start(out=place_raw[g][:], in_=place_rows[:, :, g * U_PART:(g + 1) * U_PART])
        for quad in range(P // QUADRANT):
            nc.sync.dma_start(out=key_scales[QUADRANT * quad:QUADRANT * (quad + 1), :].bitcast(I32),
                              in_=keys_scales[0, PACK * quad:PACK * (quad + 1), :].bitcast(I32)
                              .partition_broadcast(QUADRANT // PACK))
        nc.sync.dma_start(out=key_words[:].bitcast(I32), in_=keys_words[0].bitcast(I32))
        nc.sync.dma_start(out=q_raw[:], in_=query.rearrange("(p t) q -> p t q", t=PACK))
        nc.sync.dma_start(places[:], offs2)
        nc.sync.dma_start(out=size_raw[:], in_=size[0].rearrange("(p t) -> p t", t=PACK))
        val_rows = vals.rearrange("(m j) t -> m j t", j=PACK)
        for j in range(PACK):
            nc.sync.dma_start(out=planes[j][:], in_=val_rows[:, j, :])

        ident = sb.tile([P, P], F32, name="ident")
        make_identity(nc, ident[:])
        b_sb = [sb.tile([P, B_WINDOW], F32, name="b_sb%d" % h) for h in range(HALVES)]
        for h in range(HALVES):
            nc.gpsimd.memset(b_sb[h][:, U:], 0.0)

        pq_grp = sb.tile([P, Q, PACK], BF16, name="pq_grp", align_bytes=64)
        group(nc.vector.tensor_copy, pq_grp[:], pq_raw[:])
        pq_codes, pq_scales = quantize("pq", pq_grp[:], Q)
        place_grp = [sb.tile([P, U_PART, PACK], BF16, name="place_grp%d" % g, align_bytes=64) for g in range(2)]
        group(nc.vector.tensor_copy, place_grp[0][:], place_raw[0][:])
        group(nc.vector.tensor_copy, place_grp[1][:, :PLACE_ON_VECTOR, :], place_raw[1][:, :, :PLACE_ON_VECTOR])
        group(scalar_cast, place_grp[1][:, PLACE_ON_VECTOR:, :], place_raw[1][:, :, PLACE_ON_VECTOR:])
        place_mx = [quantize("place%d" % g, place_grp[g][:], U_PART) for g in range(2)]

        slot_scales = sb.tile([P, I], U8, name="slot_scales", align_bytes=64)
        nc.vector.tensor_copy(slot_scales[:], key_scales[:].indirect(slots[:]))
        slot_words = sb.tile([P, I], U16, name="slot_words", align_bytes=64)
        nc.vector.tensor_copy(slot_words[:], key_words[:].indirect(slots[:]))

        b_ps = []
        for h in range(HALVES):
            cols = slice(h * P, (h + 1) * P)
            bank = ps.tile([P, U], F32, name="b_ps%d" % h, tag="b_then_out", bufs=2)
            for g in range(2):
                nc.tensor.matmul_mx(out=bank[:, g * U_PART:(g + 1) * U_PART],
                                    lhsT=pq_codes[:, cols].bitcast(FP8X4), lhsT_scale=pq_scales[:, cols],
                                    rhs=place_mx[g][0][:].bitcast(FP8X4), rhs_scale=place_mx[g][1][:],
                                    start=True, stop=True)
            b_ps.append(bank)
        for h in range(HALVES):
            nc.scalar.copy(out=b_sb[h][:, :U], in_=b_ps[h][:])

        q_grp = sb.tile([P, Q, PACK], BF16, name="q_grp", tag="q_grp", align_bytes=64)
        group(nc.scalar.copy, q_grp[:], q_raw[:])
        b_slots0 = sb.tile([P, I], F32, name="b_slots0", align_bytes=64)
        nc.vector.tensor_copy(b_slots0[:], b_sb[0][:].indirect(places[:]))
        q_codes, q_scales = quantize("q", q_grp[:], Q)
        b_slots1 = sb.tile([P, I], F32, name="b_slots1", tag="q_grp", align_bytes=64)
        nc.vector.tensor_copy(b_slots1[:], b_sb[1][:].indirect(places[:]))
        b_slots = [b_slots0, b_slots1]
        a_ps = []
        for h in range(HALVES):
            cols = slice(h * P, (h + 1) * P)
            bank = ps.tile([P, I], F32, name="a_ps%d" % h, tag="a_then_wt", bufs=2)
            nc.tensor.matmul_mx(out=bank[:], lhsT=q_codes[:, cols].bitcast(FP8X4), lhsT_scale=q_scales[:, cols],
                                rhs=slot_words[:].bitcast(FP4X4), rhs_scale=slot_scales[:], start=True, stop=True)
            a_ps.append(bank)

        size_ps = ps.tile([P, PACK, P], F32, name="size_ps")
        for t in range(PACK):
            nc.tensor.transpose(size_ps[:, t, :], size_raw[:, t:t + 1].to_broadcast([P, P]), ident[:])

        plane0_bf16 = sb.tile([P, T], BF16, name="plane0_bf16", align_bytes=64)
        scalar_cast(plane0_bf16[:], planes[0][:])

        scores = [sb.tile([P, I], F32, name="s%d" % h, tag="s%d" % h, align_bytes=64) for h in range(HALVES)]
        neg_max = [sb.tile([P, 1], F32, name="neg_max%d" % h) for h in range(HALVES)]
        probs = [sb.tile([P, I], F32, name="p0", tag="plane0", align_bytes=64), sb.tile([P, I], F32, name="p1")]
        sums = sb.tile([P, HALVES], F32, name="sums")
        inv_sums = sb.tile([P, HALVES], F32, name="inv_sums")
        for h in range(HALVES):
            nc.vector.scalar_tensor_tensor(out=scores[h][:], in0=b_slots[h][:], scalar=1.0, in1=a_ps[h][:],
                                           op0=ALU.add, op1=ALU.mult)
        for h in range(HALVES):
            nc.vector.tensor_reduce(out=neg_max[h][:], in_=scores[h][:], axis=mybir.AxisListType.X, op=ALU.max, negate=True)
            nc.scalar.activation(out=probs[h][:], in_=scores[h][:], func=ACT.Exp, bias=neg_max[h][:],
                                 accum_out=sums[:, h:h + 1])

        v_slots0 = sb.tile([P, I], BF16, name="v_slots0", tag="s1", align_bytes=64)
        scalar_cast(v_slots0[:], plane0_bf16[:].indirect(slots[:]))

        def turn(name, by_slot, tag, bufs, grouped):
            words = by_slot[:].bitcast(F32)
            bank = ps.tile([P, 2, P], F32, name=name + "_ps", tag=tag, bufs=bufs)
            for u in range(2):
                nc.tensor.transpose(bank[:, u, :], words[:, u::2], ident[:])
            nc.scalar.copy(out=grouped.rearrange("p c t -> p (c t)").bitcast(F32).rearrange("p (c u) -> p c u", u=2),
                           in_=bank[:].rearrange("p u c -> p c u"))

        joint_grp = sb.tile([P, Q + 2 * P, PACK], BF16, name="joint_grp", tag="joint_grp", align_bytes=64)
        vt2_grp = sb.tile([P, P, PACK], BF16, name="vt2_grp", align_bytes=64)
        vt3_grp = sb.tile([P, P, PACK], BF16, name="vt3_grp", align_bytes=64)
        vt_banks = 3

        def gather_values(j, grouped):
            v_slots = sb.tile([P, I], BF16, name="v_slots%d" % j, align_bytes=64)
            nc.vector.tensor_copy(v_slots[:], planes[j][:].indirect(slots[:]))
            turn("vt%d" % j, v_slots, "vt", vt_banks, grouped)

        def weights(h):
            w = sb.tile([P, I], BF16, name="w%d" % h, align_bytes=64)
            nc.vector.scalar_tensor_tensor(out=w[:].rearrange("q (s t) -> q s t", t=PACK),
                                           in0=probs[h][:].rearrange("q (s t) -> q s t", t=PACK),
                                           scalar=inv_sums[:, h:h + 1],
                                           in1=size_ps[:].rearrange("q t s -> q s t"), op0=ALU.mult, op1=ALU.mult)
            turn("wt%d" % h, w, "a_then_wt", 2, joint_grp[:, h * P:(h + 1) * P, :])

        gather_values(1, joint_grp[:, Q + P:, :])
        turn("vt0", v_slots0, "vt", vt_banks, joint_grp[:, Q:Q + P, :])
        nc.vector.reciprocal(out=inv_sums[:], in_=sums[:])
        weights(0)
        weights(1)
        gather_values(2, vt2_grp[:])
        gather_values(3, vt3_grp[:])
        joint_codes, joint_scales = quantize("joint", joint_grp[:], Q + 2 * P, codes_tag="plane3")
        vt2_codes, vt2_scales = quantize("vt2", vt2_grp[:], P, codes_tag="joint_grp")
        vt3_codes, vt3_scales = quantize("vt3", vt3_grp[:], P)
        vt_mx = [(joint_codes[:, Q:Q + P], joint_scales[:, Q:Q + P]), (joint_codes[:, Q + P:], joint_scales[:, Q + P:]),
                 (vt2_codes[:], vt2_scales[:]), (vt3_codes[:], vt3_scales[:])]

        o01_ps = ps.tile([P, 2, Q], F32, name="o01_ps", tag="b_then_out", bufs=2)
        o2_ps = ps.tile([P, Q], F32, name="o2_ps", tag="b_then_out", bufs=2)
        o3_ps = ps.tile([P, Q], F32, name="o3_ps", tag="a_then_wt", bufs=2)
        for j, target in enumerate((o01_ps[:, 0, :], o01_ps[:, 1, :], o2_ps[:], o3_ps[:])):
            nc.tensor.matmul_mx(out=target, lhsT=vt_mx[j][0].bitcast(FP8X4), lhsT_scale=vt_mx[j][1],
                                rhs=joint_codes[:, :Q].bitcast(FP8X4), rhs_scale=joint_scales[:, :Q],
                                start=True, stop=True)
        out_rows = out_0.rearrange("(m j) q -> m j q", j=PACK)
        o_sb = sb.tile([P, PACK, Q], F32, name="o_sb")
        nc.scalar.copy(out=o_sb[:, :2, :], in_=o01_ps[:])
        nc.sync.dma_start(out=out_rows[:, :2, :], in_=o_sb[:, :2, :])
        nc.vector.tensor_copy(out=o_sb[:, 2, :], in_=o2_ps[:])
        nc.scalar.copy(out=o_sb[:, 3, :], in_=o3_ps[:])
        nc.sync.dma_start(out=out_rows[:, 2:, :], in_=o_sb[:, 2:, :])

        o_grp = sb.tile([P, Q, PACK], BF16, name="o_grp", align_bytes=64)
        group(nc.vector.tensor_copy, o_grp[:, :P, :], o_sb[:, :, :P])
        group(nc.vector.tensor_copy, o_grp[:, P:OUT_ON_VECTOR, :], o_sb[:, :, P:OUT_ON_VECTOR])
        group(nc.scalar.copy, o_grp[:, OUT_ON_VECTOR:, :], o_sb[:, :, OUT_ON_VECTOR:])
        o_codes = sb.tile([P, Q], U32, name="o_codes", align_bytes=64)
        o_scales = sb.tile([P, Q], U8, name="o_scales", align_bytes=64)
        for h in range(HALVES):
            cols = slice(h * P, (h + 1) * P)
            nc.vector.quantize_mx(out=o_codes[:, cols].bitcast(FP8X4), scales=o_scales[:, cols],
                                  in_=o_grp[:, cols, :].rearrange("p c t -> p (c t)"))
        nc.sync.dma_start(out=out_1[0].rearrange("l c r -> l (c r)").bitcast(I32), in_=o_codes[:].bitcast(I32))
        for quad, queue in enumerate((nc.sync, nc.sync, nc.scalar, nc.scalar)):
            queue.dma_start(out=out_2[0, PACK * quad:PACK * (quad + 1), :].bitcast(I32),
                            in_=o_scales[QUADRANT * quad:QUADRANT * quad + PACK, :].bitcast(I32))
